import numpy as np
import ml_dtypes


def mxq(x, axis, fmt="e4m3"):
    dtype, down = {"e4m3": (ml_dtypes.float8_e4m3fn, 7), "e5m2": (ml_dtypes.float8_e5m2, 14)}[fmt]
    v = np.moveaxis(np.asarray(x, np.float32).astype(ml_dtypes.bfloat16).astype(np.float64), axis, -1)
    blocks = v.reshape(v.shape[:-1] + (-1, 32))
    amax = np.abs(blocks).max(-1, keepdims=True)
    byte = np.maximum(np.where(amax > 0, np.frexp(amax)[1] - 1 + 127, 0) - down, 1)
    scale = np.exp2(byte - 127.0)
    codes = (blocks / scale).astype(np.float32).astype(dtype).astype(np.float64)
    return np.moveaxis((codes * scale).reshape(v.shape), -1, axis)


WIDE = False


def mx_kscale(k):
    if not WIDE:
        return np.ones(k)
    levels = np.array([10, -10, 5, -5, 0])
    if k % 512:
        return np.exp2(np.random.permutation(np.resize(levels, k // 32))).repeat(32)
    a = np.empty((k // 512, 16))
    for p in range(k // 512):
        a[p, :8] = np.random.permutation(np.resize(levels, 8))
        for g in range(8):
            far = levels[np.abs(levels - a[p, g]) >= 10]
            a[p, g + 8] = far[np.random.randint(len(far))]
    return np.exp2(a.ravel()).repeat(32)


BF16 = ml_dtypes.bfloat16


def bf(x):
    return np.asarray(x, np.float32).astype(BF16)


def f64(x):
    return np.asarray(x).astype(np.float64)


B, S, Q, C, P = 512, 1024, 2048, 512, 1024


def sigmoid(z):
    return 0.5 * (1.0 + np.tanh(0.5 * z))


def draw0():
    s, r, t = mx_kscale(S), mx_kscale(C), mx_kscale(P)
    return {"sens": bf(np.random.standard_normal((B, S)) * s),
            "w_val": bf(np.random.standard_normal((S, P)) / np.sqrt(S) / s[:, None] * t),
            "c_val": bf(0.3 * np.random.standard_normal(P) * t),
            "w_gate": bf(np.random.standard_normal((S, P)) / np.sqrt(S) / s[:, None]),
            "c_gate": bf(0.5 * np.random.standard_normal(P)),
            "feat": bf(np.random.standard_normal((Q, C)) * r),
            "w_trunk": bf(np.random.standard_normal((C, P)) / np.sqrt(C) / r[:, None]),
            "c_trunk": bf(0.3 * np.random.standard_normal(P)),
            "slope": bf(1.0 + 0.1 * np.random.standard_normal(P)),
            "amp": bf((1.0 + 0.1 * np.random.standard_normal(P)) / t),
            "dist": bf(np.random.uniform(0.3, 1.5, Q)),
            "lift": bf(0.3 * np.random.standard_normal(Q))}


def core(sens, w_val, c_val, w_gate, c_gate, feat, w_trunk, c_trunk, slope, amp, dist, lift):
    xq = mxq(f64(sens), 1, "e4m3")
    val = (xq @ mxq(f64(w_val), 0, "e4m3")) + f64(c_val)
    gate = sigmoid((xq @ mxq(f64(w_gate), 0, "e4m3")) + f64(c_gate))
    beta = val * gate
    z = (mxq(f64(feat), 1, "e4m3") @ mxq(f64(w_trunk), 0, "e4m3")) + f64(c_trunk)
    tau = f64(amp) * np.tanh(f64(slope) * z)
    field = mxq(beta, 1, "e4m3") @ mxq(tau, 1, "e4m3").T
    return f64(lift) + f64(dist) * field / np.sqrt(P)


def e4m3fn_bytes(y):
    return np.clip(np.asarray(y, np.float64), -448.0, 448.0).astype(np.float32).astype(ml_dtypes.float8_e4m3fn).view(np.uint8)


def e4m3fn_values(b):
    return np.asarray(b, np.uint8).view(ml_dtypes.float8_e4m3fn).astype(np.float64)


def setup_inputs():
    d = draw0()
    x0 = np.asarray(d['w_gate']).astype(np.float64)
    s = (np.max(np.abs(x0), axis=(1,), keepdims=True) / 448.0).astype(np.float32)
    out = {}
    for k, v in d.items():
        if k == 'w_gate':
            out['w_gate_bytes'] = e4m3fn_bytes(x0 / s.astype(np.float64))
            out['w_gate_scale'] = s
        else:
            out[k] = v
    return out


def reference(sens, w_val, c_val, w_gate_bytes, w_gate_scale, c_gate, feat, w_trunk, c_trunk, slope, amp, dist, lift):
    return core(sens, w_val, c_val, e4m3fn_values(w_gate_bytes) * w_gate_scale.astype(np.float64), c_gate, feat, w_trunk, c_trunk, slope, amp, dist, lift)

@@ -1,0 +1,394 @@
+from contextlib import ExitStack
+
+import concourse.mybir as mybir
+from concourse.masks import make_identity
+
+B, S, Q, C, P = 512, 1024, 2048, 512, 1024
+FLOPS = 2 * (2 * B * S * P + Q * C * P + B * Q * P)
+
+F32 = mybir.dt.float32
+BF16 = mybir.dt.bfloat16
+U32 = mybir.dt.uint32
+U8 = mybir.dt.uint8
+FP8 = mybir.dt.float8_e4m3fn
+FP8X4 = mybir.dt.float8_e4m3fn_x4
+ACT = mybir.ActivationFunctionType
+ALU = mybir.AluOpType
+
+PART = 128
+PACK = 4
+K_PASS = 512
+CHUNK = 512
+N_CHUNK = P // CHUNK
+Q_TILE = 512
+N_QT = Q // Q_TILE
+S_PASS = S // K_PASS
+
+
+def tile_gated_deeponet_meet_f5_kernel(
+    tc, sens, w_val, c_val, w_gate_bytes, w_gate_scale, c_gate, feat, w_trunk, c_trunk, slope, amp, dist, lift, out
+):
+    nc = tc.nc
+    with ExitStack() as ctx:
+        keep = ctx.enter_context(tc.tile_pool(name="keep", bufs=1))
+        wpool = ctx.enter_context(tc.tile_pool(name="wpool", bufs=3))
+        xpool = ctx.enter_context(tc.tile_pool(name="xpool", bufs=3))
+        widep = ctx.enter_context(tc.tile_pool(name="widep", bufs=2))
+        bigp = ctx.enter_context(tc.tile_pool(name="bigp", bufs=8))
+        taup = ctx.enter_context(tc.tile_pool(name="taup", bufs=3))
+        branchp = ctx.enter_context(tc.tile_pool(name="branchp", bufs=2))
+        outp = ctx.enter_context(tc.tile_pool(name="outp", bufs=6))
+        rowp = ctx.enter_context(tc.tile_pool(name="rowp", bufs=8))
+        ptr = ctx.enter_context(tc.psum_pool(name="ptr", bufs=2))
+        pmm = ctx.enter_context(tc.psum_pool(name="pmm", bufs=4))
+        pob = ctx.enter_context(tc.psum_pool(name="pob", bufs=2))
+        ctx.enter_context(tc.manual_schedule())
+
+        ident = keep.tile([PART, PART], F32, name="ident")
+        make_identity(nc, ident[:])
+        ident_bf = keep.tile([PART, PART], BF16, name="ident_bf")
+        nc.vector.tensor_copy(out=ident_bf[:], in_=ident[:])
+        warm = keep.tile([PART, 1], F32, name="warm")
+        nc.vector.memset(warm[:], 0.0)
+        nc.scalar.activation(out=warm[:], in_=warm[:], func=ACT.Sigmoid)
+        vecs = keep.tile([PART, 512], BF16, name="vecs")
+        nc.vector.memset(vecs[:], 0.0)
+        vecs_late = keep.tile([PART, 512], BF16, name="vecs_late")
+        nc.vector.memset(vecs_late[:], 0.0)
+
+        wtr_raw = bigp.tile([PART, PACK, P], BF16, tag="big", name="wtr_raw")
+        wtr_hbm = w_trunk.rearrange("(p j) n -> p j n", j=PACK)
+        feat_raw = keep.tile([PART, N_QT, 4, C], BF16, name="feat_raw")
+        feat_hbm = feat.rearrange("(q i p) k -> q p i k", q=N_QT, p=PART)
+        gate_raw = bigp.tile([PART, S_PASS, PACK, P], U8, tag="big", name="gate_raw")
+        gate_hbm = w_gate_bytes.rearrange("(g p j) n -> g p j n", g=S_PASS, j=PACK)
+        sens_raw = bigp.tile([PART, 4, S], BF16, tag="big", name="sens_raw")
+        sens_hbm = sens.rearrange("(i p) k -> p i k", p=PART)
+        wval_raw = []
+        for g in range(S_PASS):
+            val_pass = bigp.tile([PART, PACK, P], BF16, tag="big", name="val_pass")
+            wval_raw.append(val_pass)
+        wval_hbm = w_val.rearrange("(g p j) n -> g p j n", g=S_PASS, j=PACK)
+        gsc = keep.tile([PART, S_PASS, PACK], F32, name="gsc")
+
+        nc.sync.dma_start(out=feat_raw[:, 0, 0:2], in_=feat_hbm[0][:, 0:2])
+        nc.sync.dma_start(out=wtr_raw[:, :, 0:CHUNK], in_=wtr_hbm[:, :, 0:CHUNK])
+        nc.sync.dma_start(out=feat_raw[:, 0, 2:4], in_=feat_hbm[0][:, 2:4])
+        nc.sync.dma_start(out=gate_raw[:, 0], in_=gate_hbm[0])
+        nc.sync.dma_start(out=wtr_raw[:, :, CHUNK:P], in_=wtr_hbm[:, :, CHUNK:P])
+        nc.sync.dma_start(out=wval_raw[0][:], in_=wval_hbm[0])
+        nc.sync.dma_start(out=gate_raw[:, 1], in_=gate_hbm[1])
+        nc.sync.dma_start(out=sens_raw[:], in_=sens_hbm)
+        nc.sync.dma_start(out=wval_raw[1][:], in_=wval_hbm[1])
+        for q in range(1, N_QT):
+            nc.sync.dma_start(out=feat_raw[:, q], in_=feat_hbm[q])
+
+        nc.scalar.dma_start(out=gsc[:], in_=w_gate_scale.rearrange("(g p j) o -> p g (j o)", g=S_PASS, j=PACK))
+        for row, vec in ((4, c_trunk), (6, slope), (8, amp), (0, c_val), (2, c_gate), (10, dist), (14, lift)):
+            n = vec.shape[0] // 512
+            rows = vecs if 4 <= row < 10 else vecs_late
+            nc.gpsimd.dma_start(out=rows[row : row + n, :], in_=vec.rearrange("(r n) -> r n", n=512))
+
+        vt = keep.tile([PART, 4, 10], F32, name="vt")
+        dist_col = keep.tile([PART, 4, 4], F32, name="dist_col")
+        lift_col = keep.tile([PART, 4, 4], F32, name="lift_col")
+        tbias = keep.tile([PART, 4, 2], F32, name="tbias")
+
+        def constants():
+            pv = ptr.tile([PART, 8, PART], BF16, tag="tr", name="pv")
+            for t in range(4):
+                nc.tensor.transpose(pv[:, t, :], vecs[:, t::4], ident_bf[:])
+            nc.vector.tensor_copy(out=vt[:, :, 4:10], in_=pv[:, 0:4, 4:10])
+            nc.vector.tensor_tensor(out=tbias[:], in0=vt[:, :, 4:6], in1=vt[:, :, 6:8], op=ALU.mult)
+
+        def constants_late():
+            pv = ptr.tile([PART, 8, PART], BF16, tag="tr", name="pv")
+            for t in range(4):
+                nc.tensor.transpose(pv[:, t, :], vecs_late[:, t::4], ident_bf[:])
+            for s in range(4):
+                nc.tensor.transpose(pv[:, 4 + s, :], vecs_late[:, PART * s : PART * (s + 1)], ident_bf[:])
+            nc.vector.tensor_copy(out=vt[:, :, 0:4], in_=pv[:, 0:4, 0:4])
+            nc.vector.tensor_scalar(
+                out=dist_col[:], in0=pv[:, 4:8, 10:14], scalar1=1.0 / 32.0, scalar2=None, op0=ALU.mult
+            )
+            nc.vector.tensor_copy(out=lift_col[:], in_=pv[:, 4:8, 14:18])
+
+        def weight_chunk(raw, codes, scales, c):
+            cols = slice(c * CHUNK, (c + 1) * CHUNK)
+            grouped = wpool.tile([PART, CHUNK * PACK], BF16, tag="wgrp", name="wgrp", align_bytes=64)
+            nc.vector.tensor_copy(
+                out=grouped[:].rearrange("p (t m j) -> p t m j", t=4, j=PACK),
+                in_=raw.rearrange("p j (m t) -> p t m j", t=4),
+            )
+            return grouped, codes[:, cols], scales[:, cols]
+
+        def quant(item):
+            grouped, codes, scales = item
+            nc.vector.quantize_mx(out=codes.bitcast(FP8X4), scales=scales, in_=grouped[:])
+
+        def turned(raw, g, codes, scales, on_vector):
+            grouped = xpool.tile([PART, 512 * PACK], BF16, tag="xgrp", name="xgrp", align_bytes=64)
+            gw = grouped[:].bitcast(F32)
+            for h in range(2):
+                xt = ptr.tile([PART, 2, 2, PART], F32, tag="tr", name="xt")
+                for i in range(2):
+                    words = raw[:, 2 * h + i, K_PASS * g : K_PASS * (g + 1)].bitcast(F32)
+                    for u in range(2):
+                        nc.tensor.transpose(xt[:, i, u, :], words[:, u::2], ident[:])
+                grouped_half = gw[:, 512 * h : 512 * (h + 1)].rearrange("p (i r u) -> p i r u", i=2, u=2)
+                if h in on_vector:
+                    nc.vector.tensor_copy(out=grouped_half, in_=xt[:].rearrange("p i u r -> p i r u"))
+                else:
+                    nc.scalar.copy(out=grouped_half, in_=xt[:].rearrange("p i u r -> p i r u"))
+            return grouped, codes, scales
+
+        def mm(acc, lc, ls, rc, rs, start, stop):
+            nc.tensor.matmul_mx(
+                out=acc, lhsT=lc.bitcast(FP8X4), lhsT_scale=ls, rhs=rc.bitcast(FP8X4), rhs_scale=rs,
+                start=start, stop=stop,
+            )
+
+        wtr_codes = keep.tile([PART, P], U32, name="wtr_codes", align_bytes=64)
+        wtr_scales = keep.tile([PART, P], U8, name="wtr_scales", align_bytes=64)
+        feat_codes = keep.tile([PART, N_QT, 512], U32, name="feat_codes", align_bytes=64)
+        feat_scales = keep.tile([PART, N_QT, 512], U8, name="feat_scales", align_bytes=64)
+        gate_codes = keep.tile([PART, S_PASS, P], U32, name="gate_codes", align_bytes=64)
+        gate_scales = keep.tile([PART, S_PASS, P], U8, name="gate_scales", align_bytes=64)
+        val_codes = keep.tile([PART, S_PASS, P], U32, name="val_codes", align_bytes=64)
+        val_scales = keep.tile([PART, S_PASS, P], U8, name="val_scales", align_bytes=64)
+        sens_codes = keep.tile([PART, S_PASS, B], U32, name="sens_codes", align_bytes=64)
+        sens_scales = keep.tile([PART, S_PASS, B], U8, name="sens_scales", align_bytes=64)
+        beta_codes = keep.tile([PART, N_CHUNK, B], U32, name="beta_codes", align_bytes=64)
+        beta_scales = keep.tile([PART, N_CHUNK, B], U8, name="beta_scales", align_bytes=64)
+        tau_codes = keep.tile([PART, N_QT, N_CHUNK, Q_TILE], U32, name="tau_codes", align_bytes=64)
+        tau_scales = keep.tile([PART, N_QT, N_CHUNK, Q_TILE], U8, name="tau_scales", align_bytes=64)
+
+        def trunk_weight(c):
+            return weight_chunk(wtr_raw[:, :, c * CHUNK : (c + 1) * CHUNK], wtr_codes, wtr_scales, c)
+
+        def val_weight(g, c):
+            return weight_chunk(wval_raw[g][:, :, c * CHUNK : (c + 1) * CHUNK], val_codes[:, g, :], val_scales[:, g, :], c)
+
+        def widen(g, c, on_vector=False):
+            wide = widep.tile([PART, PACK, CHUNK], BF16, tag="wide", name="wide")
+            for j in range(PACK):
+                codes = gate_raw[:, g, j, c * CHUNK : (c + 1) * CHUNK].bitcast(FP8)
+                if on_vector:
+                    nc.vector.tensor_scalar(
+                        out=wide[:, j, :], in0=codes, scalar1=gsc[:, g, j : j + 1], scalar2=None, op0=ALU.mult
+                    )
+                else:
+                    nc.scalar.activation(out=wide[:, j, :], in_=codes, func=ACT.Copy, scale=gsc[:, g, j : j + 1])
+            return wide
+
+        def gate_weight(wide, g, c):
+            return weight_chunk(wide[:], gate_codes[:, g, :], gate_scales[:, g, :], c)
+
+        def turn_feat(q, on_vector=()):
+            return turned(feat_raw[:, q], 0, feat_codes[:, q, :], feat_scales[:, q, :], on_vector)
+
+        def turn_sens(g, on_vector=()):
+            return turned(sens_raw, g, sens_codes[:, g, :], sens_scales[:, g, :], on_vector)
+
+        def trunk(q, c):
+            th = bigp.tile([PART, 4, Q_TILE], F32, tag="big", name="th")
+            for t in range(4):
+                cols = slice(c * CHUNK + t * PART, c * CHUNK + (t + 1) * PART)
+                zp = pmm.tile([PART, Q_TILE], F32, tag="mm", name="zp")
+                mm(zp[:], wtr_codes[:, cols], wtr_scales[:, cols], feat_codes[:, q, :], feat_scales[:, q, :], True, True)
+                nc.scalar.activation(
+                    out=th[:, t, :], in_=zp[:], func=ACT.Tanh, scale=vt[:, t, 6 + c : 7 + c], bias=tbias[:, t, c : c + 1]
+                )
+            return th
+
+        def amplify(th, q, c, first=0, width=Q_TILE):
+            n = slice(first, first + width)
+            tau = taup.tile([PART, width * PACK], BF16, tag="tau", name="tau", align_bytes=64)
+            nc.vector.tensor_tensor(
+                out=tau[:].rearrange("p (n t) -> p n t", t=4),
+                in0=th[:, :, n].rearrange("p t n -> p n t"),
+                in1=vt[:, :, 8 + c].unsqueeze(1).to_broadcast([PART, width, 4]),
+                op=ALU.mult,
+            )
+            return tau, tau_codes[:, q, c, n], tau_scales[:, q, c, n]
+
+        betas = []
+        for c in range(N_CHUNK):
+            beta_tile = branchp.tile([PART, 4, B], BF16, tag="beta", name="beta_tile")
+            betas.append(beta_tile)
+
+        def branch_gate(c, t):
+            cols = slice(c * CHUNK + t * PART, c * CHUNK + (t + 1) * PART)
+            gp = pmm.tile([PART, B], F32, tag="mm", name="gp")
+            for g in range(S_PASS):
+                mm(gp[:], gate_codes[:, g, cols], gate_scales[:, g, cols], sens_codes[:, g, :], sens_scales[:, g, :], g == 0, g == S_PASS - 1)
+            sig = branchp.tile([PART, B], F32, tag="sig", name="sig")
+            nc.scalar.activation(out=sig[:], in_=gp[:], func=ACT.Sigmoid, bias=vt[:, t, 2 + c : 3 + c])
+            return sig
+
+        def branch_value(sig, c, t):
+            cols = slice(c * CHUNK + t * PART, c * CHUNK + (t + 1) * PART)
+            vp = pmm.tile([PART, B], F32, tag="mm", name="vp")
+            for g in range(S_PASS):
+                mm(vp[:], val_codes[:, g, cols], val_scales[:, g, cols], sens_codes[:, g, :], sens_scales[:, g, :], g == 0, g == S_PASS - 1)
+            nc.vector.scalar_tensor_tensor(
+                out=betas[c][:, t, :], in0=vp[:], scalar=vt[:, t, c : c + 1], in1=sig[:], op0=ALU.add, op1=ALU.mult
+            )
+
+        def beta_group(c):
+            bgrp = xpool.tile([PART, B * PACK], BF16, tag="xgrp", name="bgrp", align_bytes=64)
+            nc.vector.tensor_copy(
+                out=bgrp[:].rearrange("p (n t) -> p n t", t=4), in_=betas[c][:].rearrange("p t n -> p n t")
+            )
+            return bgrp, beta_codes[:, c, :], beta_scales[:, c, :]
+
+        def meet(q, s, on_vector=False):
+            fp = pmm.tile([PART, B], F32, tag="mm", name="fp")
+            cols = slice(PART * s, PART * (s + 1))
+            for c in range(N_CHUNK):
+                mm(fp[:], tau_codes[:, q, c, cols], tau_scales[:, q, c, cols], beta_codes[:, c, :], beta_scales[:, c, :], c == 0, c == N_CHUNK - 1)
+            o1 = outp.tile([PART, B], F32, tag="o1", name="o1")
+            if on_vector:
+                nc.vector.tensor_scalar(
+                    out=o1[:], in0=fp[:], scalar1=dist_col[:, s, q : q + 1], scalar2=lift_col[:, s, q : q + 1],
+                    op0=ALU.mult, op1=ALU.add,
+                )
+            else:
+                nc.scalar.activation(
+                    out=o1[:], in_=fp[:], func=ACT.Identity, scale=dist_col[:, s, q : q + 1], bias=lift_col[:, s, q : q + 1]
+                )
+            return o1
+
+        def store(tiles, q, i, on_vector=False, subs=(0, 1, 2, 3)):
+            width = PART * len(subs)
+            op = pob.tile([PART, width], F32, tag="ob", name="op")
+            for n, s in enumerate(subs):
+                nc.tensor.transpose(op[:, PART * n : PART * (n + 1)], tiles[n][:, PART * i : PART * (i + 1)], ident[:])
+            orow = rowp.tile([PART, width], F32, tag="orow", name="orow")
+            if on_vector:
+                nc.vector.tensor_copy(out=orow[:], in_=op[:])
+            else:
+                nc.scalar.copy(out=orow[:], in_=op[:])
+            q0 = Q_TILE * q + PART * subs[0]
+            nc.sync.dma_start(out=out[PART * i : PART * (i + 1), q0 : q0 + width], in_=orow[:])
+
+        f0 = turn_feat(0, ())
+        wt00 = trunk_weight(0)
+        quant(wt00)
+        quant(f0)
+        constants()
+        wide00 = widen(0, 0, False)
+        wt01 = trunk_weight(1)
+        wg00 = gate_weight(wide00, 0, 0)
+        th00 = trunk(0, 0)
+        wide10 = widen(1, 0, False)
+        wv00 = val_weight(0, 0)
+        quant(wg00)
+        quant(wt01)
+        quant(wv00)
+        constants_late()
+        wg10 = gate_weight(wide10, 1, 0)
+        wide11 = widen(1, 1, False)
+        wv10 = val_weight(1, 0)
+        s0 = turn_sens(0, ())
+        th01 = trunk(0, 1)
+        f1 = turn_feat(1, ())
+        wg11 = gate_weight(wide11, 1, 1)
+        quant(wv10)
+        quant(s0)
+        a00 = amplify(th00, 0, 0)
+        s1 = turn_sens(1, ())
+        quant(wg10)
+        quant(s1)
+        quant(f1)
+        wv11 = val_weight(1, 1)
+        f3 = turn_feat(3, ())
+        sig00 = branch_gate(0, 0)
+        f2 = turn_feat(2, ())
+        quant(wg11)
+        sig02 = branch_gate(0, 2)
+        quant(f3)
+        branch_value(sig00, 0, 0)
+        quant(f2)
+        branch_value(sig02, 0, 2)
+        wide01 = widen(0, 1, False)
+        wv01 = val_weight(0, 1)
+        sig03 = branch_gate(0, 3)
+        branch_value(sig03, 0, 3)
+        sig01 = branch_gate(0, 1)
+        wg01 = gate_weight(wide01, 0, 1)
+        th11 = trunk(1, 1)
+        branch_value(sig01, 0, 1)
+        th10 = trunk(1, 0)
+        quant(wg01)
+        quant(wv11)
+        sig13 = branch_gate(1, 3)
+        sig11 = branch_gate(1, 1)
+        a01 = amplify(th01, 0, 1)
+        th31 = trunk(3, 1)
+        quant(wv01)
+        bg0 = beta_group(0)
+        branch_value(sig11, 1, 1)
+        branch_value(sig13, 1, 3)
+        a10 = amplify(th10, 1, 0)
+        th21 = trunk(2, 1)
+        quant(a01)
+        sig10 = branch_gate(1, 0)
+        sig12 = branch_gate(1, 2)
+        quant(a00)
+        branch_value(sig10, 1, 0)
+        branch_value(sig12, 1, 2)
+        quant(bg0)
+        bg1 = beta_group(1)
+        th20 = trunk(2, 0)
+        th30 = trunk(3, 0)
+        quant(a10)
+        quant(bg1)
+        o00 = meet(0, 0, False)
+        a11 = amplify(th11, 1, 1)
+        o01 = meet(0, 1, False)
+        a20 = amplify(th20, 2, 0)
+        o02 = meet(0, 2, False)
+        quant(a11)
+        a21 = amplify(th21, 2, 1)
+        o03 = meet(0, 3, False)
+        quant(a20)
+        store((o00, o01, o02, o03), 0, 0, False)
+        store((o00, o01, o02, o03), 0, 1, False)
+        store((o00, o01, o02, o03), 0, 3, False)
+        quant(a21)
+        a310 = amplify(th31, 3, 1, 0, 256)
+        store((o00, o01, o02, o03), 0, 2, False)
+        o11 = meet(1, 1, False)
+        o12 = meet(1, 2, False)
+        o10 = meet(1, 0, False)
+        o13 = meet(1, 3, False)
+        store((o10, o11, o12, o13), 1, 2, False)
+        a30 = amplify(th30, 3, 0)
+        store((o10, o11, o12, o13), 1, 1, False)
+        o20 = meet(2, 0, False)
+        o22 = meet(2, 2, False)
+        store((o10, o11, o12, o13), 1, 0, False)
+        store((o10, o11, o12, o13), 1, 3, True)
+        o21 = meet(2, 1, False)
+        quant(a30)
+        o23 = meet(2, 3, False)
+        store((o20, o21, o22, o23), 2, 1, False)
+        quant(a310)
+        a311 = amplify(th31, 3, 1, 256, 256)
+        quant(a311)
+        store((o20, o21, o22, o23), 2, 2, False)
+        o30 = meet(3, 0, False)
+        store((o20, o21, o22, o23), 2, 3, False)
+        store((o20, o21, o22, o23), 2, 0, False)
+        o31 = meet(3, 1, True)
+        o33 = meet(3, 3, False)
+        store((o30, o31), 3, 0, True, (0, 1))
+        store((o30, o31), 3, 2, False, (0, 1))
+        o32 = meet(3, 2, False)
+        store((o30, o31), 3, 3, True, (0, 1))
+        store((o30, o31), 3, 1, False, (0, 1))
+        store((o32, o33), 3, 3, False, (2, 3))
+        store((o32, o33), 3, 1, False, (2, 3))
+        store((o32, o33), 3, 2, True, (2, 3))
+        store((o32, o33), 3, 0, False, (2, 3))

@@ -45,16 +45,15 @@ def tile_gated_deeponet_meet_f5_kernel(
         ctx.enter_context(tc.manual_schedule())
 
         ident = keep.tile([PART, PART], F32, name="ident")
-        make_identity(nc, ident[:])
         ident_bf = keep.tile([PART, PART], BF16, name="ident_bf")
-        nc.vector.tensor_copy(out=ident_bf[:], in_=ident[:])
         warm = keep.tile([PART, 1], F32, name="warm")
         nc.vector.memset(warm[:], 0.0)
-        nc.scalar.activation(out=warm[:], in_=warm[:], func=ACT.Sigmoid)
         vecs = keep.tile([PART, 512], BF16, name="vecs")
-        nc.vector.memset(vecs[:], 0.0)
+        nc.gpsimd.memset(vecs[:], 0.0)
         vecs_late = keep.tile([PART, 512], BF16, name="vecs_late")
-        nc.vector.memset(vecs_late[:], 0.0)
+        make_identity(nc, ident[:])
+        nc.gpsimd.memset(vecs_late[:], 0.0)
+        nc.vector.tensor_copy(out=ident_bf[:], in_=ident[:])
 
         wtr_raw = bigp.tile([PART, PACK, P], BF16, tag="big", name="wtr_raw")
         wtr_hbm = w_trunk.rearrange("(p j) n -> p j n", j=PACK)
@@ -71,23 +70,30 @@ def tile_gated_deeponet_meet_f5_kernel(
         wval_hbm = w_val.rearrange("(g p j) n -> g p j n", g=S_PASS, j=PACK)
         gsc = keep.tile([PART, S_PASS, PACK], F32, name="gsc")
 
+        def load_rows(queue, rows, first, vec):
+            n = vec.shape[0] // 512
+            queue.dma_start(out=rows[first : first + n, :], in_=vec.rearrange("(r n) -> r n", n=512))
+
+        nc.scalar.activation(out=warm[:], in_=warm[:], func=ACT.Sigmoid)
         nc.sync.dma_start(out=feat_raw[:, 0, 0:2], in_=feat_hbm[0][:, 0:2])
         nc.sync.dma_start(out=wtr_raw[:, :, 0:CHUNK], in_=wtr_hbm[:, :, 0:CHUNK])
+        load_rows(nc.sync, vecs, 4, c_trunk)
+        load_rows(nc.sync, vecs, 6, slope)
+        load_rows(nc.sync, vecs, 8, amp)
+        nc.sync.dma_start(out=gsc[:], in_=w_gate_scale.rearrange("(g p j) o -> p g (j o)", g=S_PASS, j=PACK))
         nc.sync.dma_start(out=feat_raw[:, 0, 2:4], in_=feat_hbm[0][:, 2:4])
         nc.sync.dma_start(out=gate_raw[:, 0], in_=gate_hbm[0])
         nc.sync.dma_start(out=wtr_raw[:, :, CHUNK:P], in_=wtr_hbm[:, :, CHUNK:P])
         nc.sync.dma_start(out=wval_raw[0][:], in_=wval_hbm[0])
         nc.sync.dma_start(out=gate_raw[:, 1], in_=gate_hbm[1])
         nc.sync.dma_start(out=sens_raw[:], in_=sens_hbm)
+        load_rows(nc.sync, vecs_late, 0, c_val)
+        load_rows(nc.sync, vecs_late, 2, c_gate)
+        load_rows(nc.sync, vecs_late, 10, dist)
+        load_rows(nc.sync, vecs_late, 14, lift)
         nc.sync.dma_start(out=wval_raw[1][:], in_=wval_hbm[1])
         for q in range(1, N_QT):
             nc.sync.dma_start(out=feat_raw[:, q], in_=feat_hbm[q])
-
-        nc.scalar.dma_start(out=gsc[:], in_=w_gate_scale.rearrange("(g p j) o -> p g (j o)", g=S_PASS, j=PACK))
-        for row, vec in ((4, c_trunk), (6, slope), (8, amp), (0, c_val), (2, c_gate), (10, dist), (14, lift)):
-            n = vec.shape[0] // 512
-            rows = vecs if 4 <= row < 10 else vecs_late
-            nc.gpsimd.dma_start(out=rows[row : row + n, :], in_=vec.rearrange("(r n) -> r n", n=512))
 
         vt = keep.tile([PART, 4, 10], F32, name="vt")
         dist_col = keep.tile([PART, 4, 4], F32, name="dist_col")
@@ -117,8 +123,8 @@ def tile_gated_deeponet_meet_f5_kernel(
             cols = slice(c * CHUNK, (c + 1) * CHUNK)
             grouped = wpool.tile([PART, CHUNK * PACK], BF16, tag="wgrp", name="wgrp", align_bytes=64)
             nc.vector.tensor_copy(
-                out=grouped[:].rearrange("p (t m j) -> p t m j", t=4, j=PACK),
-                in_=raw.rearrange("p j (m t) -> p t m j", t=4),
+                out=grouped[:].rearrange("p (t m j) -> p m j t", t=4, j=PACK),
+                in_=raw.rearrange("p j (m t) -> p m j t", t=4),
             )
             return grouped, codes[:, cols], scales[:, cols]
 
@@ -238,7 +244,7 @@ def tile_gated_deeponet_meet_f5_kernel(
         def beta_group(c):
             bgrp = xpool.tile([PART, B * PACK], BF16, tag="xgrp", name="bgrp", align_bytes=64)
             nc.vector.tensor_copy(
-                out=bgrp[:].rearrange("p (n t) -> p n t", t=4), in_=betas[c][:].rearrange("p t n -> p n t")
+                out=bgrp[:].rearrange("p (n i t) -> p n t i", i=4, t=4), in_=betas[c][:].rearrange("p t (n i) -> p n t i", i=4)
             )
             return bgrp, beta_codes[:, c, :], beta_scales[:, c, :]
 
@@ -274,121 +280,121 @@ def tile_gated_deeponet_meet_f5_kernel(
 
         f0 = turn_feat(0, ())
         wt00 = trunk_weight(0)
-        quant(wt00)
-        quant(f0)
-        constants()
         wide00 = widen(0, 0, False)
+        constants()
+        quant(f0)
+        quant(wt00)
         wt01 = trunk_weight(1)
         wg00 = gate_weight(wide00, 0, 0)
         th00 = trunk(0, 0)
-        wide10 = widen(1, 0, False)
-        wv00 = val_weight(0, 0)
-        quant(wg00)
-        quant(wt01)
-        quant(wv00)
-        constants_late()
-        wg10 = gate_weight(wide10, 1, 0)
-        wide11 = widen(1, 1, False)
-        wv10 = val_weight(1, 0)
-        s0 = turn_sens(0, ())
-        th01 = trunk(0, 1)
-        f1 = turn_feat(1, ())
-        wg11 = gate_weight(wide11, 1, 1)
-        quant(wv10)
-        quant(s0)
-        a00 = amplify(th00, 0, 0)
-        s1 = turn_sens(1, ())
-        quant(wg10)
-        quant(s1)
-        quant(f1)
-        wv11 = val_weight(1, 1)
-        f3 = turn_feat(3, ())
-        sig00 = branch_gate(0, 0)
-        f2 = turn_feat(2, ())
-        quant(wg11)
-        sig02 = branch_gate(0, 2)
-        quant(f3)
-        branch_value(sig00, 0, 0)
-        quant(f2)
-        branch_value(sig02, 0, 2)
-        wide01 = widen(0, 1, False)
         wv01 = val_weight(0, 1)
-        sig03 = branch_gate(0, 3)
-        branch_value(sig03, 0, 3)
-        sig01 = branch_gate(0, 1)
-        wg01 = gate_weight(wide01, 0, 1)
-        th11 = trunk(1, 1)
-        branch_value(sig01, 0, 1)
-        th10 = trunk(1, 0)
-        quant(wg01)
-        quant(wv11)
-        sig13 = branch_gate(1, 3)
-        sig11 = branch_gate(1, 1)
-        a01 = amplify(th01, 0, 1)
-        th31 = trunk(3, 1)
+        quant(wt01)
+        wide10 = widen(1, 0, False)
+        s0 = turn_sens(0, ())
+        quant(wg00)
         quant(wv01)
-        bg0 = beta_group(0)
-        branch_value(sig11, 1, 1)
-        branch_value(sig13, 1, 3)
+        th01 = trunk(0, 1)
+        wv00 = val_weight(0, 0)
+        f1 = turn_feat(1, ())
+        wv10 = val_weight(1, 0)
+        wg10 = gate_weight(wide10, 1, 0)
+        quant(wv00)
+        quant(wv10)
+        s1 = turn_sens(1, ())
+        quant(f1)
+        wide01 = widen(0, 1, False)
+        quant(wg10)
+        quant(s0)
+        constants_late()
+        quant(s1)
+        f3 = turn_feat(3, ())
+        sig03 = branch_gate(0, 3)
+        a00 = amplify(th00, 0, 0)
+        wide11 = widen(1, 1, False)
+        branch_value(sig03, 0, 3)
+        a01 = amplify(th01, 0, 1)
+        th10 = trunk(1, 0)
+        sig01 = branch_gate(0, 1)
+        wv11 = val_weight(1, 1)
+        wg11 = gate_weight(wide11, 1, 1)
+        branch_value(sig01, 0, 1)
+        f2 = turn_feat(2, ())
+        wg01 = gate_weight(wide01, 0, 1)
+        quant(f2)
+        sig00 = branch_gate(0, 0)
+        quant(wg11)
+        quant(wg01)
+        sig02 = branch_gate(0, 2)
+        th11 = trunk(1, 1)
+        branch_value(sig00, 0, 0)
+        branch_value(sig02, 0, 2)
+        quant(wv11)
         a10 = amplify(th10, 1, 0)
-        th21 = trunk(2, 1)
-        quant(a01)
         sig10 = branch_gate(1, 0)
-        sig12 = branch_gate(1, 2)
-        quant(a00)
-        branch_value(sig10, 1, 0)
-        branch_value(sig12, 1, 2)
-        quant(bg0)
-        bg1 = beta_group(1)
         th20 = trunk(2, 0)
+        branch_value(sig10, 1, 0)
+        sig12 = branch_gate(1, 2)
+        sig11 = branch_gate(1, 1)
+        quant(f3)
+        branch_value(sig12, 1, 2)
+        quant(a01)
+        branch_value(sig11, 1, 1)
+        bg0 = beta_group(0)
+        sig13 = branch_gate(1, 3)
+        th31 = trunk(3, 1)
+        branch_value(sig13, 1, 3)
+        th21 = trunk(2, 1)
+        quant(a00)
+        bg1 = beta_group(1)
+        quant(bg0)
         th30 = trunk(3, 0)
-        quant(a10)
         quant(bg1)
+        o01 = meet(0, 1, False)
+        o02 = meet(0, 2, False)
         o00 = meet(0, 0, False)
         a11 = amplify(th11, 1, 1)
-        o01 = meet(0, 1, False)
-        a20 = amplify(th20, 2, 0)
-        o02 = meet(0, 2, False)
-        quant(a11)
-        a21 = amplify(th21, 2, 1)
         o03 = meet(0, 3, False)
+        quant(a10)
+        quant(a11)
+        o12 = meet(1, 2, False)
+        a21 = amplify(th21, 2, 1)
+        o11 = meet(1, 1, True)
+        store((o00, o01, o02, o03), 0, 2, False)
+        store((o00, o01, o02, o03), 0, 3, False)
+        store((o00, o01, o02, o03), 0, 1, False)
+        a20 = amplify(th20, 2, 0)
+        quant(a21)
         quant(a20)
         store((o00, o01, o02, o03), 0, 0, False)
-        store((o00, o01, o02, o03), 0, 1, False)
-        store((o00, o01, o02, o03), 0, 3, False)
-        quant(a21)
-        a310 = amplify(th31, 3, 1, 0, 256)
-        store((o00, o01, o02, o03), 0, 2, False)
-        o11 = meet(1, 1, False)
-        o12 = meet(1, 2, False)
         o10 = meet(1, 0, False)
         o13 = meet(1, 3, False)
+        store((o10, o11, o12, o13), 1, 0, False)
+        store((o10, o11, o12, o13), 1, 3, False)
+        store((o10, o11, o12, o13), 1, 1, False)
         store((o10, o11, o12, o13), 1, 2, False)
         a30 = amplify(th30, 3, 0)
-        store((o10, o11, o12, o13), 1, 1, False)
         o20 = meet(2, 0, False)
         o22 = meet(2, 2, False)
-        store((o10, o11, o12, o13), 1, 0, False)
-        store((o10, o11, o12, o13), 1, 3, True)
+        a310 = amplify(th31, 3, 1, 0, 256)
         o21 = meet(2, 1, False)
-        quant(a30)
         o23 = meet(2, 3, False)
+        store((o20, o21, o22, o23), 2, 0, False)
+        quant(a30)
         store((o20, o21, o22, o23), 2, 1, False)
         quant(a310)
-        a311 = amplify(th31, 3, 1, 256, 256)
-        quant(a311)
-        store((o20, o21, o22, o23), 2, 2, False)
         o30 = meet(3, 0, False)
+        a311 = amplify(th31, 3, 1, 256, 256)
+        store((o20, o21, o22, o23), 2, 2, False)
+        quant(a311)
         store((o20, o21, o22, o23), 2, 3, False)
-        store((o20, o21, o22, o23), 2, 0, False)
-        o31 = meet(3, 1, True)
+        o32 = meet(3, 2, True)
         o33 = meet(3, 3, False)
-        store((o30, o31), 3, 0, True, (0, 1))
-        store((o30, o31), 3, 2, False, (0, 1))
-        o32 = meet(3, 2, False)
-        store((o30, o31), 3, 3, True, (0, 1))
-        store((o30, o31), 3, 1, False, (0, 1))
-        store((o32, o33), 3, 3, False, (2, 3))
+        o31 = meet(3, 1, True)
         store((o32, o33), 3, 1, False, (2, 3))
-        store((o32, o33), 3, 2, True, (2, 3))
+        store((o32, o33), 3, 3, True, (2, 3))
+        store((o30, o31), 3, 1, True, (0, 1))
+        store((o30, o31), 3, 0, False, (0, 1))
+        store((o32, o33), 3, 2, False, (2, 3))
+        store((o30, o31), 3, 2, True, (0, 1))
+        store((o30, o31), 3, 3, True, (0, 1))
         store((o32, o33), 3, 0, False, (2, 3))

@@ -211,9 +211,9 @@ def tile_gated_deeponet_meet_f5_kernel(
             n = slice(first, first + width)
             tau = taup.tile([PART, width * PACK], BF16, tag="tau", name="tau", align_bytes=64)
             nc.vector.tensor_tensor(
-                out=tau[:].rearrange("p (n t) -> p n t", t=4),
-                in0=th[:, :, n].rearrange("p t n -> p n t"),
-                in1=vt[:, :, 8 + c].unsqueeze(1).to_broadcast([PART, width, 4]),
+                out=tau[:].rearrange("p (n i t) -> p n t i", i=4, t=4),
+                in0=th[:, :, n].rearrange("p t (n i) -> p n t i", i=4),
+                in1=vt[:, :, 8 + c].unsqueeze(1).unsqueeze(3).to_broadcast([PART, width // 4, 4, 4]),
                 op=ALU.mult,
             )
             return tau, tau_codes[:, q, c, n], tau_scales[:, q, c, n]

@@ -100,17 +100,27 @@ def tile_gated_deeponet_meet_f5_kernel(
         lift_col = keep.tile([PART, 4, 4], F32, name="lift_col")
         tbias = keep.tile([PART, 4, 2], F32, name="tbias")
 
+        def by_tile(rows):
+            tiled = xpool.tile([PART, 512], BF16, tag="tiled", name="tiled")
+            nc.scalar.copy(
+                out=tiled[:].rearrange("p (t b e) -> p t b e", t=4, e=8),
+                in_=rows[:].rearrange("p (b t e) -> p t b e", t=4, e=8),
+            )
+            return tiled
+
         def constants():
+            turned_rows = by_tile(vecs)
             pv = ptr.tile([PART, 8, PART], BF16, tag="tr", name="pv")
             for t in range(4):
-                nc.tensor.transpose(pv[:, t, :], vecs[:, t::4], ident_bf[:])
+                nc.tensor.transpose(pv[:, t, :], turned_rows[:, PART * t : PART * (t + 1)], ident_bf[:])
             nc.vector.tensor_copy(out=vt[:, :, 4:10], in_=pv[:, 0:4, 4:10])
             nc.vector.tensor_tensor(out=tbias[:], in0=vt[:, :, 4:6], in1=vt[:, :, 6:8], op=ALU.mult)
 
         def constants_late():
+            turned_rows = by_tile(vecs_late)
             pv = ptr.tile([PART, 8, PART], BF16, tag="tr", name="pv")
             for t in range(4):
-                nc.tensor.transpose(pv[:, t, :], vecs_late[:, t::4], ident_bf[:])
+                nc.tensor.transpose(pv[:, t, :], turned_rows[:, PART * t : PART * (t + 1)], ident_bf[:])
             for s in range(4):
                 nc.tensor.transpose(pv[:, 4 + s, :], vecs_late[:, PART * s : PART * (s + 1)], ident_bf[:])
             nc.vector.tensor_copy(out=vt[:, :, 0:4], in_=pv[:, 0:4, 0:4])
@@ -123,8 +133,8 @@ def tile_gated_deeponet_meet_f5_kernel(
             cols = slice(c * CHUNK, (c + 1) * CHUNK)
             grouped = wpool.tile([PART, CHUNK * PACK], BF16, tag="wgrp", name="wgrp", align_bytes=64)
             nc.vector.tensor_copy(
-                out=grouped[:].rearrange("p (t m j) -> p m j t", t=4, j=PACK),
-                in_=raw.rearrange("p j (m t) -> p m j t", t=4),
+                out=grouped[:].rearrange("p (t b e j) -> p b t e j", t=4, e=8, j=PACK),
+                in_=raw.rearrange("p j (b t e) -> p b t e j", t=4, e=8),
             )
             return grouped, codes[:, cols], scales[:, cols]
 
@@ -278,123 +288,123 @@ def tile_gated_deeponet_meet_f5_kernel(
             q0 = Q_TILE * q + PART * subs[0]
             nc.sync.dma_start(out=out[PART * i : PART * (i + 1), q0 : q0 + width], in_=orow[:])
 
-        f0 = turn_feat(0, ())
         wt00 = trunk_weight(0)
-        wide00 = widen(0, 0, False)
+        f0 = turn_feat(0, (1,))
         constants()
         quant(f0)
         quant(wt00)
+        wide00 = widen(0, 0, False)
         wt01 = trunk_weight(1)
-        wg00 = gate_weight(wide00, 0, 0)
-        th00 = trunk(0, 0)
-        wv01 = val_weight(0, 1)
-        quant(wt01)
-        wide10 = widen(1, 0, False)
-        s0 = turn_sens(0, ())
-        quant(wg00)
-        quant(wv01)
-        th01 = trunk(0, 1)
-        wv00 = val_weight(0, 0)
-        f1 = turn_feat(1, ())
-        wv10 = val_weight(1, 0)
-        wg10 = gate_weight(wide10, 1, 0)
-        quant(wv00)
-        quant(wv10)
-        s1 = turn_sens(1, ())
-        quant(f1)
         wide01 = widen(0, 1, False)
-        quant(wg10)
-        quant(s0)
-        constants_late()
-        quant(s1)
-        f3 = turn_feat(3, ())
-        sig03 = branch_gate(0, 3)
-        a00 = amplify(th00, 0, 0)
+        wg00 = gate_weight(wide00, 0, 0)
         wide11 = widen(1, 1, False)
+        s0 = turn_sens(0, ())
+        wv00 = val_weight(0, 0)
+        quant(wt01)
+        quant(wg00)
+        s1 = turn_sens(1, ())
+        wg11 = gate_weight(wide11, 1, 1)
+        wv10 = val_weight(1, 0)
+        quant(wv00)
+        quant(wg11)
+        wg01 = gate_weight(wide01, 0, 1)
+        quant(s0)
+        quant(wv10)
+        wv01 = val_weight(0, 1)
+        th00 = trunk(0, 0)
+        f1 = turn_feat(1, ())
+        quant(wg01)
+        f2 = turn_feat(2, (1,))
+        quant(s1)
+        constants_late()
+        wide10 = widen(1, 0, False)
+        quant(f2)
+        wg10 = gate_weight(wide10, 1, 0)
+        quant(wv01)
+        quant(wg10)
+        f3 = turn_feat(3, ())
+        wv11 = val_weight(1, 1)
+        quant(f3)
+        th20 = trunk(2, 0)
+        sig03 = branch_gate(0, 3)
         branch_value(sig03, 0, 3)
+        sig00 = branch_gate(0, 0)
+        quant(wv11)
+        sig02 = branch_gate(0, 2)
+        branch_value(sig00, 0, 0)
+        th01 = trunk(0, 1)
+        a00 = amplify(th00, 0, 0)
+        branch_value(sig02, 0, 2)
+        sig10 = branch_gate(1, 0)
+        quant(f1)
+        sig12 = branch_gate(1, 2)
+        branch_value(sig10, 1, 0)
         a01 = amplify(th01, 0, 1)
         th10 = trunk(1, 0)
-        sig01 = branch_gate(0, 1)
-        wv11 = val_weight(1, 1)
-        wg11 = gate_weight(wide11, 1, 1)
-        branch_value(sig01, 0, 1)
-        f2 = turn_feat(2, ())
-        wg01 = gate_weight(wide01, 0, 1)
-        quant(f2)
-        sig00 = branch_gate(0, 0)
-        quant(wg11)
-        quant(wg01)
-        sig02 = branch_gate(0, 2)
-        th11 = trunk(1, 1)
-        branch_value(sig00, 0, 0)
-        branch_value(sig02, 0, 2)
-        quant(wv11)
-        a10 = amplify(th10, 1, 0)
-        sig10 = branch_gate(1, 0)
-        th20 = trunk(2, 0)
-        branch_value(sig10, 1, 0)
-        sig12 = branch_gate(1, 2)
-        sig11 = branch_gate(1, 1)
-        quant(f3)
         branch_value(sig12, 1, 2)
+        sig11 = branch_gate(1, 1)
+        sig01 = branch_gate(0, 1)
         quant(a01)
-        branch_value(sig11, 1, 1)
-        bg0 = beta_group(0)
-        sig13 = branch_gate(1, 3)
-        th31 = trunk(3, 1)
-        branch_value(sig13, 1, 3)
-        th21 = trunk(2, 1)
         quant(a00)
+        branch_value(sig11, 1, 1)
+        th30 = trunk(3, 0)
+        a10 = amplify(th10, 1, 0)
+        sig13 = branch_gate(1, 3)
+        branch_value(sig01, 0, 1)
+        branch_value(sig13, 1, 3)
+        bg0 = beta_group(0)
+        th11 = trunk(1, 1)
         bg1 = beta_group(1)
         quant(bg0)
-        th30 = trunk(3, 0)
+        th21 = trunk(2, 1)
         quant(bg1)
-        o01 = meet(0, 1, False)
-        o02 = meet(0, 2, False)
-        o00 = meet(0, 0, False)
-        a11 = amplify(th11, 1, 1)
         o03 = meet(0, 3, False)
+        a11 = amplify(th11, 1, 1)
+        o01 = meet(0, 1, False)
         quant(a10)
-        quant(a11)
-        o12 = meet(1, 2, False)
-        a21 = amplify(th21, 2, 1)
-        o11 = meet(1, 1, True)
-        store((o00, o01, o02, o03), 0, 2, False)
-        store((o00, o01, o02, o03), 0, 3, False)
-        store((o00, o01, o02, o03), 0, 1, False)
         a20 = amplify(th20, 2, 0)
-        quant(a21)
+        o00 = meet(0, 0, False)
+        o02 = meet(0, 2, False)
+        th31 = trunk(3, 1)
+        store((o00, o01, o02, o03), 0, 1, False)
+        quant(a11)
+        a21 = amplify(th21, 2, 1)
         quant(a20)
-        store((o00, o01, o02, o03), 0, 0, False)
+        quant(a21)
+        store((o00, o01, o02, o03), 0, 2, False)
+        o11 = meet(1, 1, False)
+        o12 = meet(1, 2, False)
+        store((o00, o01, o02, o03), 0, 3, False)
+        store((o00, o01, o02, o03), 0, 0, True)
+        a30 = amplify(th30, 3, 0)
         o10 = meet(1, 0, False)
         o13 = meet(1, 3, False)
-        store((o10, o11, o12, o13), 1, 0, False)
-        store((o10, o11, o12, o13), 1, 3, False)
-        store((o10, o11, o12, o13), 1, 1, False)
-        store((o10, o11, o12, o13), 1, 2, False)
-        a30 = amplify(th30, 3, 0)
         o20 = meet(2, 0, False)
-        o22 = meet(2, 2, False)
-        a310 = amplify(th31, 3, 1, 0, 256)
-        o21 = meet(2, 1, False)
-        o23 = meet(2, 3, False)
-        store((o20, o21, o22, o23), 2, 0, False)
-        quant(a30)
-        store((o20, o21, o22, o23), 2, 1, False)
-        quant(a310)
-        o30 = meet(3, 0, False)
+        store((o10, o11, o12, o13), 1, 0, False)
+        store((o10, o11, o12, o13), 1, 1, False)
         a311 = amplify(th31, 3, 1, 256, 256)
-        store((o20, o21, o22, o23), 2, 2, False)
+        o22 = meet(2, 2, False)
+        store((o10, o11, o12, o13), 1, 2, False)
+        quant(a30)
         quant(a311)
+        store((o10, o11, o12, o13), 1, 3, True)
+        o23 = meet(2, 3, False)
+        o21 = meet(2, 1, False)
+        a310 = amplify(th31, 3, 1, 0, 256)
+        o32 = meet(3, 2, False)
+        store((o20, o21, o22, o23), 2, 1, False)
         store((o20, o21, o22, o23), 2, 3, False)
-        o32 = meet(3, 2, True)
-        o33 = meet(3, 3, False)
+        o33 = meet(3, 3, True)
+        store((o20, o21, o22, o23), 2, 0, False)
+        quant(a310)
+        store((o20, o21, o22, o23), 2, 2, True)
+        o30 = meet(3, 0, True)
+        store((o32, o33), 3, 2, False, (2, 3))
+        store((o32, o33), 3, 0, True, (2, 3))
         o31 = meet(3, 1, True)
-        store((o32, o33), 3, 1, False, (2, 3))
-        store((o32, o33), 3, 3, True, (2, 3))
+        store((o32, o33), 3, 3, False, (2, 3))
+        store((o32, o33), 3, 1, True, (2, 3))
         store((o30, o31), 3, 1, True, (0, 1))
         store((o30, o31), 3, 0, False, (0, 1))
-        store((o32, o33), 3, 2, False, (2, 3))
         store((o30, o31), 3, 2, True, (0, 1))
-        store((o30, o31), 3, 3, True, (0, 1))
-        store((o32, o33), 3, 0, False, (2, 3))
+        store((o30, o31), 3, 3, False, (0, 1))

@@ -39,9 +39,8 @@ def tile_gated_deeponet_meet_f5_kernel(
         branchp = ctx.enter_context(tc.tile_pool(name="branchp", bufs=2))
         outp = ctx.enter_context(tc.tile_pool(name="outp", bufs=6))
         rowp = ctx.enter_context(tc.tile_pool(name="rowp", bufs=8))
-        ptr = ctx.enter_context(tc.psum_pool(name="ptr", bufs=2))
+        ptr = ctx.enter_context(tc.psum_pool(name="ptr", bufs=4))
         pmm = ctx.enter_context(tc.psum_pool(name="pmm", bufs=4))
-        pob = ctx.enter_context(tc.psum_pool(name="pob", bufs=2))
         ctx.enter_context(tc.manual_schedule())
 
         ident = keep.tile([PART, PART], F32, name="ident")
@@ -75,23 +74,23 @@ def tile_gated_deeponet_meet_f5_kernel(
             queue.dma_start(out=rows[first : first + n, :], in_=vec.rearrange("(r n) -> r n", n=512))
 
         nc.scalar.activation(out=warm[:], in_=warm[:], func=ACT.Sigmoid)
-        nc.sync.dma_start(out=feat_raw[:, 0, 0:2], in_=feat_hbm[0][:, 0:2])
         nc.sync.dma_start(out=wtr_raw[:, :, 0:CHUNK], in_=wtr_hbm[:, :, 0:CHUNK])
+        nc.sync.dma_start(out=feat_raw[:, 0, 0:2], in_=feat_hbm[0][:, 0:2])
+        nc.sync.dma_start(out=feat_raw[:, 0, 2:4], in_=feat_hbm[0][:, 2:4])
+        nc.sync.dma_start(out=gate_raw[:, 0], in_=gate_hbm[0])
         load_rows(nc.sync, vecs, 4, c_trunk)
         load_rows(nc.sync, vecs, 6, slope)
         load_rows(nc.sync, vecs, 8, amp)
         nc.sync.dma_start(out=gsc[:], in_=w_gate_scale.rearrange("(g p j) o -> p g (j o)", g=S_PASS, j=PACK))
-        nc.sync.dma_start(out=feat_raw[:, 0, 2:4], in_=feat_hbm[0][:, 2:4])
-        nc.sync.dma_start(out=gate_raw[:, 0], in_=gate_hbm[0])
         nc.sync.dma_start(out=wtr_raw[:, :, CHUNK:P], in_=wtr_hbm[:, :, CHUNK:P])
         nc.sync.dma_start(out=wval_raw[0][:], in_=wval_hbm[0])
         nc.sync.dma_start(out=gate_raw[:, 1], in_=gate_hbm[1])
         nc.sync.dma_start(out=sens_raw[:], in_=sens_hbm)
+        nc.sync.dma_start(out=wval_raw[1][:], in_=wval_hbm[1])
         load_rows(nc.sync, vecs_late, 0, c_val)
         load_rows(nc.sync, vecs_late, 2, c_gate)
         load_rows(nc.sync, vecs_late, 10, dist)
         load_rows(nc.sync, vecs_late, 14, lift)
-        nc.sync.dma_start(out=wval_raw[1][:], in_=wval_hbm[1])
         for q in range(1, N_QT):
             nc.sync.dma_start(out=feat_raw[:, q], in_=feat_hbm[q])
 
@@ -277,7 +276,7 @@ def tile_gated_deeponet_meet_f5_kernel(
 
         def store(tiles, q, i, on_vector=False, subs=(0, 1, 2, 3)):
             width = PART * len(subs)
-            op = pob.tile([PART, width], F32, tag="ob", name="op")
+            op = ptr.tile([PART, width], F32, tag="tr", name="op")
             for n, s in enumerate(subs):
                 nc.tensor.transpose(op[:, PART * n : PART * (n + 1)], tiles[n][:, PART * i : PART * (i + 1)], ident[:])
             orow = rowp.tile([PART, width], F32, tag="orow", name="orow")
@@ -289,122 +288,122 @@ def tile_gated_deeponet_meet_f5_kernel(
             nc.sync.dma_start(out=out[PART * i : PART * (i + 1), q0 : q0 + width], in_=orow[:])
 
         wt00 = trunk_weight(0)
-        f0 = turn_feat(0, (1,))
-        constants()
-        quant(f0)
+        f0 = turn_feat(0, ())
         quant(wt00)
-        wide00 = widen(0, 0, False)
+        quant(f0)
+        constants()
         wt01 = trunk_weight(1)
-        wide01 = widen(0, 1, False)
+        wide00 = widen(0, 0, False)
         wg00 = gate_weight(wide00, 0, 0)
-        wide11 = widen(1, 1, False)
-        s0 = turn_sens(0, ())
         wv00 = val_weight(0, 0)
         quant(wt01)
-        quant(wg00)
-        s1 = turn_sens(1, ())
-        wg11 = gate_weight(wide11, 1, 1)
-        wv10 = val_weight(1, 0)
+        th00 = trunk(0, 0)
+        wide01 = widen(0, 1, False)
+        wide10 = widen(1, 0, False)
         quant(wv00)
-        quant(wg11)
+        wv01 = val_weight(0, 1)
+        s1 = turn_sens(1, ())
+        quant(wg00)
+        s0 = turn_sens(0, ())
+        quant(wv01)
+        wv10 = val_weight(1, 0)
+        f2 = turn_feat(2, ())
+        wg10 = gate_weight(wide10, 1, 0)
+        quant(s1)
         wg01 = gate_weight(wide01, 0, 1)
         quant(s0)
-        quant(wv10)
-        wv01 = val_weight(0, 1)
-        th00 = trunk(0, 0)
-        f1 = turn_feat(1, ())
-        quant(wg01)
-        f2 = turn_feat(2, (1,))
-        quant(s1)
-        constants_late()
-        wide10 = widen(1, 0, False)
-        quant(f2)
-        wg10 = gate_weight(wide10, 1, 0)
-        quant(wv01)
-        quant(wg10)
         f3 = turn_feat(3, ())
-        wv11 = val_weight(1, 1)
-        quant(f3)
-        th20 = trunk(2, 0)
-        sig03 = branch_gate(0, 3)
-        branch_value(sig03, 0, 3)
-        sig00 = branch_gate(0, 0)
-        quant(wv11)
+        quant(wg10)
+        quant(wg01)
+        constants_late()
+        wide11 = widen(1, 1, False)
+        f1 = turn_feat(1, ())
+        quant(wv10)
         sig02 = branch_gate(0, 2)
-        branch_value(sig00, 0, 0)
-        th01 = trunk(0, 1)
+        sig00 = branch_gate(0, 0)
+        quant(f3)
         a00 = amplify(th00, 0, 0)
         branch_value(sig02, 0, 2)
-        sig10 = branch_gate(1, 0)
         quant(f1)
-        sig12 = branch_gate(1, 2)
-        branch_value(sig10, 1, 0)
-        a01 = amplify(th01, 0, 1)
-        th10 = trunk(1, 0)
-        branch_value(sig12, 1, 2)
-        sig11 = branch_gate(1, 1)
-        sig01 = branch_gate(0, 1)
-        quant(a01)
-        quant(a00)
-        branch_value(sig11, 1, 1)
+        wg11 = gate_weight(wide11, 1, 1)
+        th01 = trunk(0, 1)
+        sig03 = branch_gate(0, 3)
+        branch_value(sig00, 0, 0)
+        wv11 = val_weight(1, 1)
         th30 = trunk(3, 0)
-        a10 = amplify(th10, 1, 0)
-        sig13 = branch_gate(1, 3)
+        quant(wg11)
+        branch_value(sig03, 0, 3)
+        quant(f2)
+        sig01 = branch_gate(0, 1)
         branch_value(sig01, 0, 1)
-        branch_value(sig13, 1, 3)
-        bg0 = beta_group(0)
         th11 = trunk(1, 1)
-        bg1 = beta_group(1)
-        quant(bg0)
+        quant(wv11)
+        a01 = amplify(th01, 0, 1)
+        sig12 = branch_gate(1, 2)
+        sig10 = branch_gate(1, 0)
+        branch_value(sig12, 1, 2)
+        bg0 = beta_group(0)
         th21 = trunk(2, 1)
-        quant(bg1)
-        o03 = meet(0, 3, False)
+        branch_value(sig10, 1, 0)
+        sig11 = branch_gate(1, 1)
+        quant(a01)
+        sig13 = branch_gate(1, 3)
+        quant(a00)
+        th10 = trunk(1, 0)
         a11 = amplify(th11, 1, 1)
-        o01 = meet(0, 1, False)
-        quant(a10)
-        a20 = amplify(th20, 2, 0)
-        o00 = meet(0, 0, False)
-        o02 = meet(0, 2, False)
+        branch_value(sig13, 1, 3)
+        branch_value(sig11, 1, 1)
+        th20 = trunk(2, 0)
         th31 = trunk(3, 1)
-        store((o00, o01, o02, o03), 0, 1, False)
+        quant(bg0)
+        bg1 = beta_group(1)
         quant(a11)
+        quant(bg1)
+        o02 = meet(0, 2, False)
+        o00 = meet(0, 0, False)
+        a10 = amplify(th10, 1, 0)
+        o01 = meet(0, 1, False)
+        a20 = amplify(th20, 2, 0)
+        o03 = meet(0, 3, False)
+        store((o00, o01, o02, o03), 0, 1, False)
+        quant(a10)
+        store((o00, o01, o02, o03), 0, 0, False)
         a21 = amplify(th21, 2, 1)
         quant(a20)
-        quant(a21)
         store((o00, o01, o02, o03), 0, 2, False)
-        o11 = meet(1, 1, False)
-        o12 = meet(1, 2, False)
+        quant(a21)
         store((o00, o01, o02, o03), 0, 3, False)
-        store((o00, o01, o02, o03), 0, 0, True)
-        a30 = amplify(th30, 3, 0)
-        o10 = meet(1, 0, False)
         o13 = meet(1, 3, False)
-        o20 = meet(2, 0, False)
-        store((o10, o11, o12, o13), 1, 0, False)
-        store((o10, o11, o12, o13), 1, 1, False)
-        a311 = amplify(th31, 3, 1, 256, 256)
-        o22 = meet(2, 2, False)
-        store((o10, o11, o12, o13), 1, 2, False)
-        quant(a30)
-        quant(a311)
-        store((o10, o11, o12, o13), 1, 3, True)
-        o23 = meet(2, 3, False)
-        o21 = meet(2, 1, False)
+        o12 = meet(1, 2, False)
+        a30 = amplify(th30, 3, 0)
         a310 = amplify(th31, 3, 1, 0, 256)
-        o32 = meet(3, 2, False)
-        store((o20, o21, o22, o23), 2, 1, False)
-        store((o20, o21, o22, o23), 2, 3, False)
-        o33 = meet(3, 3, True)
-        store((o20, o21, o22, o23), 2, 0, False)
+        o11 = meet(1, 1, False)
+        o10 = meet(1, 0, False)
+        o20 = meet(2, 0, False)
+        o22 = meet(2, 2, False)
+        quant(a30)
+        store((o10, o11, o12, o13), 1, 0, False)
+        store((o10, o11, o12, o13), 1, 2, False)
         quant(a310)
-        store((o20, o21, o22, o23), 2, 2, True)
+        store((o10, o11, o12, o13), 1, 3, False)
+        store((o10, o11, o12, o13), 1, 1, True)
+        o21 = meet(2, 1, False)
+        a311 = amplify(th31, 3, 1, 256, 256)
+        quant(a311)
+        o23 = meet(2, 3, False)
         o30 = meet(3, 0, True)
-        store((o32, o33), 3, 2, False, (2, 3))
-        store((o32, o33), 3, 0, True, (2, 3))
+        store((o20, o21, o22, o23), 2, 3, False)
+        store((o20, o21, o22, o23), 2, 0, False)
+        store((o20, o21, o22, o23), 2, 1, False)
+        store((o20, o21, o22, o23), 2, 2, False)
+        o32 = meet(3, 2, False)
+        o33 = meet(3, 3, True)
         o31 = meet(3, 1, True)
+        store((o32, o33), 3, 1, False, (2, 3))
+        store((o32, o33), 3, 2, True, (2, 3))
         store((o32, o33), 3, 3, False, (2, 3))
-        store((o32, o33), 3, 1, True, (2, 3))
-        store((o30, o31), 3, 1, True, (0, 1))
-        store((o30, o31), 3, 0, False, (0, 1))
-        store((o30, o31), 3, 2, True, (0, 1))
         store((o30, o31), 3, 3, False, (0, 1))
+        store((o30, o31), 3, 0, True, (0, 1))
+        store((o30, o31), 3, 2, False, (0, 1))
+        store((o32, o33), 3, 0, True, (2, 3))
+        store((o30, o31), 3, 1, False, (0, 1))

from contextlib import ExitStack

import concourse.mybir as mybir
from concourse.masks import make_identity

B, S, Q, C, P = 512, 1024, 2048, 512, 1024
FLOPS = 2 * (2 * B * S * P + Q * C * P + B * Q * P)

F32 = mybir.dt.float32
BF16 = mybir.dt.bfloat16
U32 = mybir.dt.uint32
U8 = mybir.dt.uint8
FP8 = mybir.dt.float8_e4m3fn
FP8X4 = mybir.dt.float8_e4m3fn_x4
ACT = mybir.ActivationFunctionType
ALU = mybir.AluOpType

PART = 128
PACK = 4
K_PASS = 512
CHUNK = 512
N_CHUNK = P // CHUNK
Q_TILE = 512
N_QT = Q // Q_TILE
S_PASS = S // K_PASS


def tile_gated_deeponet_meet_f5_kernel(
    tc, sens, w_val, c_val, w_gate_bytes, w_gate_scale, c_gate, feat, w_trunk, c_trunk, slope, amp, dist, lift, out
):
    nc = tc.nc
    with ExitStack() as ctx:
        keep = ctx.enter_context(tc.tile_pool(name="keep", bufs=1))
        wpool = ctx.enter_context(tc.tile_pool(name="wpool", bufs=3))
        xpool = ctx.enter_context(tc.tile_pool(name="xpool", bufs=3))
        widep = ctx.enter_context(tc.tile_pool(name="widep", bufs=2))
        bigp = ctx.enter_context(tc.tile_pool(name="bigp", bufs=8))
        taup = ctx.enter_context(tc.tile_pool(name="taup", bufs=3))
        branchp = ctx.enter_context(tc.tile_pool(name="branchp", bufs=2))
        outp = ctx.enter_context(tc.tile_pool(name="outp", bufs=6))
        rowp = ctx.enter_context(tc.tile_pool(name="rowp", bufs=8))
        ptr = ctx.enter_context(tc.psum_pool(name="ptr", bufs=4))
        pmm = ctx.enter_context(tc.psum_pool(name="pmm", bufs=4))
        ctx.enter_context(tc.manual_schedule())

        ident = keep.tile([PART, PART], F32, name="ident")
        ident_bf = keep.tile([PART, PART], BF16, name="ident_bf")
        warm = keep.tile([PART, 1], F32, name="warm")
        nc.vector.memset(warm[:], 0.0)
        vecs = keep.tile([PART, 512], BF16, name="vecs")
        nc.gpsimd.memset(vecs[:], 0.0)
        vecs_late = keep.tile([PART, 512], BF16, name="vecs_late")
        make_identity(nc, ident[:])
        nc.gpsimd.memset(vecs_late[:], 0.0)
        nc.vector.tensor_copy(out=ident_bf[:], in_=ident[:])

        wtr_raw = bigp.tile([PART, PACK, P], BF16, tag="big", name="wtr_raw")
        wtr_hbm = w_trunk.rearrange("(p j) n -> p j n", j=PACK)
        feat_raw = keep.tile([PART, N_QT, 4, C], BF16, name="feat_raw")
        feat_hbm = feat.rearrange("(q i p) k -> q p i k", q=N_QT, p=PART)
        gate_raw = bigp.tile([PART, S_PASS, PACK, P], U8, tag="big", name="gate_raw")
        gate_hbm = w_gate_bytes.rearrange("(g p j) n -> g p j n", g=S_PASS, j=PACK)
        sens_raw = bigp.tile([PART, 4, S], BF16, tag="big", name="sens_raw")
        sens_hbm = sens.rearrange("(i p) k -> p i k", p=PART)
        wval_raw = []
        for g in range(S_PASS):
            val_pass = bigp.tile([PART, PACK, P], BF16, tag="big", name="val_pass")
            wval_raw.append(val_pass)
        wval_hbm = w_val.rearrange("(g p j) n -> g p j n", g=S_PASS, j=PACK)
        gsc = keep.tile([PART, S_PASS, PACK], F32, name="gsc")

        def load_rows(queue, rows, first, vec):
            n = vec.shape[0] // 512
            queue.dma_start(out=rows[first : first + n, :], in_=vec.rearrange("(r n) -> r n", n=512))

        nc.scalar.activation(out=warm[:], in_=warm[:], func=ACT.Sigmoid)
        nc.sync.dma_start(out=wtr_raw[:, :, 0:CHUNK], in_=wtr_hbm[:, :, 0:CHUNK])
        nc.sync.dma_start(out=feat_raw[:, 0, 0:2], in_=feat_hbm[0][:, 0:2])
        nc.sync.dma_start(out=feat_raw[:, 0, 2:4], in_=feat_hbm[0][:, 2:4])
        nc.sync.dma_start(out=gate_raw[:, 0], in_=gate_hbm[0])
        load_rows(nc.sync, vecs, 4, c_trunk)
        load_rows(nc.sync, vecs, 6, slope)
        load_rows(nc.sync, vecs, 8, amp)
        nc.sync.dma_start(out=gsc[:], in_=w_gate_scale.rearrange("(g p j) o -> p g (j o)", g=S_PASS, j=PACK))
        nc.sync.dma_start(out=wtr_raw[:, :, CHUNK:P], in_=wtr_hbm[:, :, CHUNK:P])
        nc.sync.dma_start(out=wval_raw[0][:], in_=wval_hbm[0])
        nc.sync.dma_start(out=gate_raw[:, 1], in_=gate_hbm[1])
        nc.sync.dma_start(out=sens_raw[:], in_=sens_hbm)
        nc.sync.dma_start(out=wval_raw[1][:], in_=wval_hbm[1])
        load_rows(nc.sync, vecs_late, 0, c_val)
        load_rows(nc.sync, vecs_late, 2, c_gate)
        load_rows(nc.sync, vecs_late, 10, dist)
        load_rows(nc.sync, vecs_late, 14, lift)
        for q in range(1, N_QT):
            nc.sync.dma_start(out=feat_raw[:, q], in_=feat_hbm[q])

        vt = keep.tile([PART, 4, 10], F32, name="vt")
        dist_col = keep.tile([PART, 4, 4], F32, name="dist_col")
        lift_col = keep.tile([PART, 4, 4], F32, name="lift_col")
        tbias = keep.tile([PART, 4, 2], F32, name="tbias")

        def by_tile(rows):
            tiled = xpool.tile([PART, 512], BF16, tag="tiled", name="tiled")
            nc.scalar.copy(
                out=tiled[:].rearrange("p (t b e) -> p t b e", t=4, e=8),
                in_=rows[:].rearrange("p (b t e) -> p t b e", t=4, e=8),
            )
            return tiled

        def constants():
            turned_rows = by_tile(vecs)
            pv = ptr.tile([PART, 8, PART], BF16, tag="tr", name="pv")
            for t in range(4):
                nc.tensor.transpose(pv[:, t, :], turned_rows[:, PART * t : PART * (t + 1)], ident_bf[:])
            nc.vector.tensor_copy(out=vt[:, :, 4:10], in_=pv[:, 0:4, 4:10])
            nc.vector.tensor_tensor(out=tbias[:], in0=vt[:, :, 4:6], in1=vt[:, :, 6:8], op=ALU.mult)

        def constants_late():
            turned_rows = by_tile(vecs_late)
            pv = ptr.tile([PART, 8, PART], BF16, tag="tr", name="pv")
            for t in range(4):
                nc.tensor.transpose(pv[:, t, :], turned_rows[:, PART * t : PART * (t + 1)], ident_bf[:])
            for s in range(4):
                nc.tensor.transpose(pv[:, 4 + s, :], vecs_late[:, PART * s : PART * (s + 1)], ident_bf[:])
            nc.vector.tensor_copy(out=vt[:, :, 0:4], in_=pv[:, 0:4, 0:4])
            nc.vector.tensor_scalar(
                out=dist_col[:], in0=pv[:, 4:8, 10:14], scalar1=1.0 / 32.0, scalar2=None, op0=ALU.mult
            )
            nc.vector.tensor_copy(out=lift_col[:], in_=pv[:, 4:8, 14:18])

        def weight_chunk(raw, codes, scales, c):
            cols = slice(c * CHUNK, (c + 1) * CHUNK)
            grouped = wpool.tile([PART, CHUNK * PACK], BF16, tag="wgrp", name="wgrp", align_bytes=64)
            nc.vector.tensor_copy(
                out=grouped[:].rearrange("p (t b e j) -> p b t e j", t=4, e=8, j=PACK),
                in_=raw.rearrange("p j (b t e) -> p b t e j", t=4, e=8),
            )
            return grouped, codes[:, cols], scales[:, cols]

        def quant(item):
            grouped, codes, scales = item
            nc.vector.quantize_mx(out=codes.bitcast(FP8X4), scales=scales, in_=grouped[:])

        def turned(raw, g, codes, scales, on_vector):
            grouped = xpool.tile([PART, 512 * PACK], BF16, tag="xgrp", name="xgrp", align_bytes=64)
            gw = grouped[:].bitcast(F32)
            for h in range(2):
                xt = ptr.tile([PART, 2, 2, PART], F32, tag="tr", name="xt")
                for i in range(2):
                    words = raw[:, 2 * h + i, K_PASS * g : K_PASS * (g + 1)].bitcast(F32)
                    for u in range(2):
                        nc.tensor.transpose(xt[:, i, u, :], words[:, u::2], ident[:])
                grouped_half = gw[:, 512 * h : 512 * (h + 1)].rearrange("p (i r u) -> p i r u", i=2, u=2)
                if h in on_vector:
                    nc.vector.tensor_copy(out=grouped_half, in_=xt[:].rearrange("p i u r -> p i r u"))
                else:
                    nc.scalar.copy(out=grouped_half, in_=xt[:].rearrange("p i u r -> p i r u"))
            return grouped, codes, scales

        def mm(acc, lc, ls, rc, rs, start, stop):
            nc.tensor.matmul_mx(
                out=acc, lhsT=lc.bitcast(FP8X4), lhsT_scale=ls, rhs=rc.bitcast(FP8X4), rhs_scale=rs,
                start=start, stop=stop,
            )

        wtr_codes = keep.tile([PART, P], U32, name="wtr_codes", align_bytes=64)
        wtr_scales = keep.tile([PART, P], U8, name="wtr_scales", align_bytes=64)
        feat_codes = keep.tile([PART, N_QT, 512], U32, name="feat_codes", align_bytes=64)
        feat_scales = keep.tile([PART, N_QT, 512], U8, name="feat_scales", align_bytes=64)
        gate_codes = keep.tile([PART, S_PASS, P], U32, name="gate_codes", align_bytes=64)
        gate_scales = keep.tile([PART, S_PASS, P], U8, name="gate_scales", align_bytes=64)
        val_codes = keep.tile([PART, S_PASS, P], U32, name="val_codes", align_bytes=64)
        val_scales = keep.tile([PART, S_PASS, P], U8, name="val_scales", align_bytes=64)
        sens_codes = keep.tile([PART, S_PASS, B], U32, name="sens_codes", align_bytes=64)
        sens_scales = keep.tile([PART, S_PASS, B], U8, name="sens_scales", align_bytes=64)
        beta_codes = keep.tile([PART, N_CHUNK, B], U32, name="beta_codes", align_bytes=64)
        beta_scales = keep.tile([PART, N_CHUNK, B], U8, name="beta_scales", align_bytes=64)
        tau_codes = keep.tile([PART, N_QT, N_CHUNK, Q_TILE], U32, name="tau_codes", align_bytes=64)
        tau_scales = keep.tile([PART, N_QT, N_CHUNK, Q_TILE], U8, name="tau_scales", align_bytes=64)

        def trunk_weight(c):
            return weight_chunk(wtr_raw[:, :, c * CHUNK : (c + 1) * CHUNK], wtr_codes, wtr_scales, c)

        def val_weight(g, c):
            return weight_chunk(wval_raw[g][:, :, c * CHUNK : (c + 1) * CHUNK], val_codes[:, g, :], val_scales[:, g, :], c)

        def widen(g, c, on_vector=False):
            wide = widep.tile([PART, PACK, CHUNK], BF16, tag="wide", name="wide")
            for j in range(PACK):
                codes = gate_raw[:, g, j, c * CHUNK : (c + 1) * CHUNK].bitcast(FP8)
                if on_vector:
                    nc.vector.tensor_scalar(
                        out=wide[:, j, :], in0=codes, scalar1=gsc[:, g, j : j + 1], scalar2=None, op0=ALU.mult
                    )
                else:
                    nc.scalar.activation(out=wide[:, j, :], in_=codes, func=ACT.Copy, scale=gsc[:, g, j : j + 1])
            return wide

        def gate_weight(wide, g, c):
            return weight_chunk(wide[:], gate_codes[:, g, :], gate_scales[:, g, :], c)

        def turn_feat(q, on_vector=()):
            return turned(feat_raw[:, q], 0, feat_codes[:, q, :], feat_scales[:, q, :], on_vector)

        def turn_sens(g, on_vector=()):
            return turned(sens_raw, g, sens_codes[:, g, :], sens_scales[:, g, :], on_vector)

        def trunk(q, c):
            th = bigp.tile([PART, 4, Q_TILE], F32, tag="big", name="th")
            for t in range(4):
                cols = slice(c * CHUNK + t * PART, c * CHUNK + (t + 1) * PART)
                zp = pmm.tile([PART, Q_TILE], F32, tag="mm", name="zp")
                mm(zp[:], wtr_codes[:, cols], wtr_scales[:, cols], feat_codes[:, q, :], feat_scales[:, q, :], True, True)
                nc.scalar.activation(
                    out=th[:, t, :], in_=zp[:], func=ACT.Tanh, scale=vt[:, t, 6 + c : 7 + c], bias=tbias[:, t, c : c + 1]
                )
            return th

        def amplify(th, q, c, first=0, width=Q_TILE):
            n = slice(first, first + width)
            tau = taup.tile([PART, width * PACK], BF16, tag="tau", name="tau", align_bytes=64)
            nc.vector.tensor_tensor(
                out=tau[:].rearrange("p (n i t) -> p n t i", i=4, t=4),
                in0=th[:, :, n].rearrange("p t (n i) -> p n t i", i=4),
                in1=vt[:, :, 8 + c].unsqueeze(1).unsqueeze(3).to_broadcast([PART, width // 4, 4, 4]),
                op=ALU.mult,
            )
            return tau, tau_codes[:, q, c, n], tau_scales[:, q, c, n]

        betas = []
        for c in range(N_CHUNK):
            beta_tile = branchp.tile([PART, 4, B], BF16, tag="beta", name="beta_tile")
            betas.append(beta_tile)

        def branch_gate(c, t):
            cols = slice(c * CHUNK + t * PART, c * CHUNK + (t + 1) * PART)
            gp = pmm.tile([PART, B], F32, tag="mm", name="gp")
            for g in range(S_PASS):
                mm(gp[:], gate_codes[:, g, cols], gate_scales[:, g, cols], sens_codes[:, g, :], sens_scales[:, g, :], g == 0, g == S_PASS - 1)
            sig = branchp.tile([PART, B], F32, tag="sig", name="sig")
            nc.scalar.activation(out=sig[:], in_=gp[:], func=ACT.Sigmoid, bias=vt[:, t, 2 + c : 3 + c])
            return sig

        def branch_value(sig, c, t):
            cols = slice(c * CHUNK + t * PART, c * CHUNK + (t + 1) * PART)
            vp = pmm.tile([PART, B], F32, tag="mm", name="vp")
            for g in range(S_PASS):
                mm(vp[:], val_codes[:, g, cols], val_scales[:, g, cols], sens_codes[:, g, :], sens_scales[:, g, :], g == 0, g == S_PASS - 1)
            nc.vector.scalar_tensor_tensor(
                out=betas[c][:, t, :], in0=vp[:], scalar=vt[:, t, c : c + 1], in1=sig[:], op0=ALU.add, op1=ALU.mult
            )

        def beta_group(c):
            bgrp = xpool.tile([PART, B * PACK], BF16, tag="xgrp", name="bgrp", align_bytes=64)
            nc.vector.tensor_copy(
                out=bgrp[:].rearrange("p (n i t) -> p n t i", i=4, t=4), in_=betas[c][:].rearrange("p t (n i) -> p n t i", i=4)
            )
            return bgrp, beta_codes[:, c, :], beta_scales[:, c, :]

        def meet(q, s, on_vector=False):
            fp = pmm.tile([PART, B], F32, tag="mm", name="fp")
            cols = slice(PART * s, PART * (s + 1))
            for c in range(N_CHUNK):
                mm(fp[:], tau_codes[:, q, c, cols], tau_scales[:, q, c, cols], beta_codes[:, c, :], beta_scales[:, c, :], c == 0, c == N_CHUNK - 1)
            o1 = outp.tile([PART, B], F32, tag="o1", name="o1")
            if on_vector:
                nc.vector.tensor_scalar(
                    out=o1[:], in0=fp[:], scalar1=dist_col[:, s, q : q + 1], scalar2=lift_col[:, s, q : q + 1],
                    op0=ALU.mult, op1=ALU.add,
                )
            else:
                nc.scalar.activation(
                    out=o1[:], in_=fp[:], func=ACT.Identity, scale=dist_col[:, s, q : q + 1], bias=lift_col[:, s, q : q + 1]
                )
            return o1

        def store(tiles, q, i, on_vector=False, subs=(0, 1, 2, 3)):
            width = PART * len(subs)
            op = ptr.tile([PART, width], F32, tag="tr", name="op")
            for n, s in enumerate(subs):
                nc.tensor.transpose(op[:, PART * n : PART * (n + 1)], tiles[n][:, PART * i : PART * (i + 1)], ident[:])
            orow = rowp.tile([PART, width], F32, tag="orow", name="orow")
            if on_vector:
                nc.vector.tensor_copy(out=orow[:], in_=op[:])
            else:
                nc.scalar.copy(out=orow[:], in_=op[:])
            q0 = Q_TILE * q + PART * subs[0]
            nc.sync.dma_start(out=out[PART * i : PART * (i + 1), q0 : q0 + width], in_=orow[:])

        wt00 = trunk_weight(0)
        f0 = turn_feat(0, ())
        quant(wt00)
        quant(f0)
        constants()
        wt01 = trunk_weight(1)
        wide00 = widen(0, 0, False)
        wg00 = gate_weight(wide00, 0, 0)
        wv00 = val_weight(0, 0)
        quant(wt01)
        th00 = trunk(0, 0)
        wide01 = widen(0, 1, False)
        wide10 = widen(1, 0, False)
        quant(wv00)
        wv01 = val_weight(0, 1)
        s1 = turn_sens(1, ())
        quant(wg00)
        s0 = turn_sens(0, ())
        quant(wv01)
        wv10 = val_weight(1, 0)
        f2 = turn_feat(2, ())
        wg10 = gate_weight(wide10, 1, 0)
        quant(s1)
        wg01 = gate_weight(wide01, 0, 1)
        quant(s0)
        f3 = turn_feat(3, ())
        quant(wg10)
        quant(wg01)
        constants_late()
        wide11 = widen(1, 1, False)
        f1 = turn_feat(1, ())
        quant(wv10)
        sig02 = branch_gate(0, 2)
        sig00 = branch_gate(0, 0)
        quant(f3)
        a00 = amplify(th00, 0, 0)
        branch_value(sig02, 0, 2)
        quant(f1)
        wg11 = gate_weight(wide11, 1, 1)
        th01 = trunk(0, 1)
        sig03 = branch_gate(0, 3)
        branch_value(sig00, 0, 0)
        wv11 = val_weight(1, 1)
        th30 = trunk(3, 0)
        quant(wg11)
        branch_value(sig03, 0, 3)
        quant(f2)
        sig01 = branch_gate(0, 1)
        branch_value(sig01, 0, 1)
        th11 = trunk(1, 1)
        quant(wv11)
        a01 = amplify(th01, 0, 1)
        sig12 = branch_gate(1, 2)
        sig10 = branch_gate(1, 0)
        branch_value(sig12, 1, 2)
        bg0 = beta_group(0)
        th21 = trunk(2, 1)
        branch_value(sig10, 1, 0)
        sig11 = branch_gate(1, 1)
        quant(a01)
        sig13 = branch_gate(1, 3)
        quant(a00)
        th10 = trunk(1, 0)
        a11 = amplify(th11, 1, 1)
        branch_value(sig13, 1, 3)
        branch_value(sig11, 1, 1)
        th20 = trunk(2, 0)
        th31 = trunk(3, 1)
        quant(bg0)
        bg1 = beta_group(1)
        quant(a11)
        quant(bg1)
        o02 = meet(0, 2, False)
        o00 = meet(0, 0, False)
        a10 = amplify(th10, 1, 0)
        o01 = meet(0, 1, False)
        a20 = amplify(th20, 2, 0)
        o03 = meet(0, 3, False)
        store((o00, o01, o02, o03), 0, 1, False)
        quant(a10)
        store((o00, o01, o02, o03), 0, 0, False)
        a21 = amplify(th21, 2, 1)
        quant(a20)
        store((o00, o01, o02, o03), 0, 2, False)
        quant(a21)
        store((o00, o01, o02, o03), 0, 3, False)
        o13 = meet(1, 3, False)
        o12 = meet(1, 2, False)
        a30 = amplify(th30, 3, 0)
        a310 = amplify(th31, 3, 1, 0, 256)
        o11 = meet(1, 1, False)
        o10 = meet(1, 0, False)
        o20 = meet(2, 0, False)
        o22 = meet(2, 2, False)
        quant(a30)
        store((o10, o11, o12, o13), 1, 0, False)
        store((o10, o11, o12, o13), 1, 2, False)
        quant(a310)
        store((o10, o11, o12, o13), 1, 3, False)
        store((o10, o11, o12, o13), 1, 1, True)
        o21 = meet(2, 1, False)
        a311 = amplify(th31, 3, 1, 256, 256)
        quant(a311)
        o23 = meet(2, 3, False)
        o30 = meet(3, 0, True)
        store((o20, o21, o22, o23), 2, 3, False)
        store((o20, o21, o22, o23), 2, 0, False)
        store((o20, o21, o22, o23), 2, 1, False)
        store((o20, o21, o22, o23), 2, 2, False)
        o32 = meet(3, 2, False)
        o33 = meet(3, 3, True)
        o31 = meet(3, 1, True)
        store((o32, o33), 3, 1, False, (2, 3))
        store((o32, o33), 3, 2, True, (2, 3))
        store((o32, o33), 3, 3, False, (2, 3))
        store((o30, o31), 3, 3, False, (0, 1))
        store((o30, o31), 3, 0, True, (0, 1))
        store((o30, o31), 3, 2, False, (0, 1))
        store((o32, o33), 3, 0, True, (2, 3))
        store((o30, o31), 3, 1, False, (0, 1))
